import numpy as np
import ml_dtypes


def mxq(x, axis, fmt="e4m3"):
    dtype, down = {"e4m3": (ml_dtypes.float8_e4m3fn, 7), "e5m2": (ml_dtypes.float8_e5m2, 14)}[fmt]
    v = np.moveaxis(np.asarray(x, np.float32).astype(ml_dtypes.bfloat16).astype(np.float64), axis, -1)
    blocks = v.reshape(v.shape[:-1] + (-1, 32))
    amax = np.abs(blocks).max(-1, keepdims=True)
    byte = np.maximum(np.where(amax > 0, np.frexp(amax)[1] - 1 + 127, 0) - down, 1)
    scale = np.exp2(byte - 127.0)
    codes = (blocks / scale).astype(np.float32).astype(dtype).astype(np.float64)
    return np.moveaxis((codes * scale).reshape(v.shape), -1, axis)


WIDE = False


def mx_kscale(k):
    if not WIDE:
        return np.ones(k)
    levels = np.array([10, -10, 5, -5, 0])
    if k % 512:
        return np.exp2(np.random.permutation(np.resize(levels, k // 32))).repeat(32)
    a = np.empty((k // 512, 16))
    for p in range(k // 512):
        a[p, :8] = np.random.permutation(np.resize(levels, 8))
        for g in range(8):
            far = levels[np.abs(levels - a[p, g]) >= 10]
            a[p, g + 8] = far[np.random.randint(len(far))]
    return np.exp2(a.ravel()).repeat(32)


def f64(x):
    return np.asarray(x).astype(np.float64)


def striped(idx):
    return np.tile(idx.reshape(-1, 16).T, (8, 1)).astype(np.uint16)


def unstriped(offs):
    return offs[:16].T.reshape(-1).astype(np.int64)


E2M1 = np.array([0.0, 0.5, 1.0, 1.5, 2.0, 3.0, 4.0, 6.0, -0.0, -0.5, -1.0, -1.5, -2.0, -3.0, -4.0, -6.0])


def pack_weight(w, fmt):
    k, n = w.shape
    w = f64(np.asarray(w, np.float32).astype(ml_dtypes.bfloat16)).reshape(k // 32, 32, n)
    amax = np.abs(w).max(1)
    if fmt == "e4m3":
        byte = np.frexp(amax)[1] - 1 + 127 - 7
    else:
        mant, ex = np.frexp(amax / 6.0)
        byte = np.where(mant > 0.5, ex, ex - 1) + 127
    byte = np.clip(np.where(amax > 0, byte, 1), 1, 254)
    scaled = (w * np.exp2(127.0 - byte)[:, None, :]).reshape(k, n).astype(np.float32)
    by_word = np.ascontiguousarray(scaled.reshape(k // 512, 128, 4, n).transpose(0, 1, 3, 2))
    if fmt == "e4m3":
        words = by_word.astype(ml_dtypes.float8_e4m3fn).view(np.uint8)
    else:
        c = by_word.astype(ml_dtypes.float4_e2m1fn).view(np.uint8) & 0xF
        words = (c[..., 0::2] | (c[..., 1::2] << 4)).reshape(k // 512, 128, 2 * n)
    return np.ascontiguousarray(words), np.ascontiguousarray(byte.astype(np.uint8).reshape(k // 512, 16, n))


def unpack_weight(words, scales, fmt):
    g, _, n = scales.shape
    words = np.ascontiguousarray(words).reshape(g, 128, n, -1)
    if fmt == "e4m3":
        vals = words.view(ml_dtypes.float8_e4m3fn).astype(np.float64)
    else:
        nib = np.empty((g, 128, n, 4), np.uint8)
        nib[..., 0::2] = words & 0xF
        nib[..., 1::2] = words >> 4
        vals = E2M1[nib]
    vals = vals * np.repeat(np.exp2(scales.astype(np.float64) - 127.0), 8, axis=1)[..., None]
    return vals.transpose(0, 1, 3, 2).reshape(g * 512, n)


def gelu(v):
    return 0.5 * v * (1.0 + np.tanh(np.sqrt(2.0 / np.pi) * (v + 0.044715 * v**3)))


def striped8(idx):
    return np.concatenate([v.reshape(-1, 16).T for v in idx]).astype(np.uint16)


def unstriped8(offs):
    return np.stack([offs[16 * g:16 * g + 16].T.reshape(-1) for g in range(8)]).astype(np.int64)


def heads(h, wgt, idx8):
    r = np.arange(h.shape[0])
    return wgt[r // 4 % 128] * h[r[:, None], idx8[r % 512 // 64]]


def put_heads(h, wgs, idx8, t2):
    r = np.arange(h.shape[0])
    page = np.zeros((h.shape[0], t2))
    page[r[:, None], idx8[r % 512 // 64]] = wgs[r // 4 % 128] * h
    return page


K, T, S, P, T2, H, N = 1024, 2048, 1024, 1024, 2048, 512, 384


def setup_inputs():
    n = np.random.standard_normal
    s = mx_kscale(K)[:, None]
    u = mx_kscale(H)[:, None]
    d = {}
    d["tab_words"], d["tab_scales"] = pack_weight(n((K, T)) * s, "e4m3")
    d["w1"] = (0.55 * n((K, H)) / K ** 0.5 / s).astype(np.float32)
    d["w2_words"], d["w2_scales"] = pack_weight(0.55 * n((K, H)) / K ** 0.5 / s, "e2m1")
    d["gain"] = (np.exp(0.3 * n(H)) * u[:, 0]).astype(np.float32)
    d["wgs"] = np.repeat(np.random.uniform(0.5, 2.0, (8, S)), 16, axis=0).astype(np.float32)
    d["wgt"] = np.repeat(np.random.uniform(0.5, 2.0, (8, P)), 16, axis=0).astype(np.float32)
    d["prick"] = (0.8 * n((H, P)) * u).astype(np.float32)
    d["w3"] = (0.7 * n((H, N)) / H ** 0.5 / u).astype(np.float32)
    d["w4_words"], d["w4_scales"] = pack_weight(0.7 * n((H, N)) / H ** 0.5 / u, "e2m1")
    d["offs"] = striped(np.random.permutation(T)[:S])
    d["offs2"] = striped8(np.stack([np.random.permutation(T2)[:S] for _ in range(8)]))
    d["offs3"] = striped8(np.stack([np.random.permutation(T2)[:P] for _ in range(8)]))
    return d


def reference(tab_words, tab_scales, w1, w2_words, w2_scales, gain, wgs, wgt, prick,
              w3, w4_words, w4_scales, offs, offs2, offs3):
    v = unpack_weight(tab_words, tab_scales, "e4m3")[:, unstriped(offs)]
    a1 = mxq(f64(w1), 0, "e4m3").T @ v
    a2 = unpack_weight(w2_words, w2_scales, "e2m1").T @ v
    h = f64(gain)[:, None] * (np.cos(a1) - np.sin(a2))
    page = put_heads(h, f64(wgs), unstriped8(offs2), T2)
    x = heads(page, f64(wgt), unstriped8(offs3))
    z = mxq(x - f64(prick), 0, "e4m3")
    y1 = mxq(f64(w3), 0, "e4m3").T @ z
    y2 = unpack_weight(w4_words, w4_scales, "e2m1").T @ z
    return y1 * y2 + y1

@@ -1,0 +1,285 @@
+import math
+from contextlib import ExitStack
+
+import concourse.mybir as mybir
+from concourse.masks import make_identity
+
+K, T, S, M, T2, H, N = 1024, 2048, 1024, 1024, 2048, 512, 384
+FLOPS = 2 * 2 * K * H * S + 2 * 2 * H * N * M
+
+F32 = mybir.dt.float32
+BF16 = mybir.dt.bfloat16
+I32 = mybir.dt.int32
+U32 = mybir.dt.uint32
+U16 = mybir.dt.uint16
+U8 = mybir.dt.uint8
+FP8X4 = mybir.dt.float8_e4m3fn_x4
+FP4X4 = mybir.dt.float4_e2m1fn_x4
+ALU = mybir.AluOpType
+ACT = mybir.ActivationFunctionType
+
+P = 128
+PACK = 4
+PASSES = K // (P * PACK)
+PICK = 256
+BLOCKS = S // P
+TURN = 2.0 * math.pi
+CHUNKS = (256, 256, 256, 128, 128)
+AHEAD = 4
+
+
+def tile_list_bobbin_path_features_kernel(
+    tc, tab_words, tab_scales, w1, w2_words, w2_scales, gain, wgs, wgt, prick,
+    w3, w4_words, w4_scales, offs, offs2, offs3, out,
+):
+    nc = tc.nc
+    with ExitStack() as ctx:
+        lists = ctx.enter_context(tc.tile_pool(name="lists", bufs=1))
+        keep = ctx.enter_context(tc.tile_pool(name="keep", bufs=1))
+        ring = ctx.enter_context(tc.tile_pool(name="ring", bufs=3))
+        psum = ctx.enter_context(tc.psum_pool(name="psum", bufs=1))
+
+        def load_scale_rows(queue, plane, rows, passes):
+            words = rows.bitcast(I32)
+            for quad in range(4):
+                queue.dma_start(
+                    out=plane[32 * quad : 32 * quad + 4, :].bitcast(I32).rearrange("r (a n) -> r a n", a=passes),
+                    in_=words[:, 4 * quad : 4 * quad + 4, :].rearrange("a r n -> r a n"),
+                )
+
+        def interleave(copy, grouped, planes):
+            copy(
+                out=grouped.rearrange("p (c i) t -> p c t i", i=4),
+                in_=planes.rearrange("p t (c i) -> p c t i", i=4),
+            )
+
+        idx = lists.tile([P, S // 16], U16, name="idx")
+        idx2 = lists.tile([P, S // 16], U16, name="idx2")
+        idx3 = lists.tile([P, M // 16], U16, name="idx3")
+
+        tab_plane = keep.tile([P, PASSES * T], U8, name="tab_plane", align_bytes=64)
+        w2_plane = keep.tile([P, PASSES * H], U8, name="w2_plane", align_bytes=64)
+        w4_plane = keep.tile([P, N], U8, name="w4_plane", align_bytes=64)
+        for plane in (tab_plane, w2_plane, w4_plane):
+            nc.vector.memset(plane[:].bitcast(I32), 0)
+
+        nc.sync.dma_start(idx[:], offs)
+        load_scale_rows(nc.scalar, tab_plane, tab_scales, PASSES)
+        tab = []
+        for a in range(PASSES):
+            words = keep.tile([P, T], I32, name=f"tab{a}", align_bytes=64)
+            nc.sync.dma_start(out=words[:], in_=tab_words[a].rearrange("p t i -> p (t i)").bitcast(I32))
+            tab.append(words)
+        w2_codes = keep.tile([P, PASSES * 2 * H], U8, name="w2_codes", align_bytes=64)
+        nc.sync.dma_start(
+            out=w2_codes[:].bitcast(I32).rearrange("p (a n) -> p a n", a=PASSES),
+            in_=w2_words.bitcast(I32).rearrange("a p n -> p a n"),
+        )
+        load_scale_rows(nc.scalar, w2_plane, w2_scales, PASSES)
+        half = H // 2
+        w1_raw = {}
+        for a in range(PASSES):
+            for u in range(2):
+                raw = keep.tile([P, PACK, half], F32, name=f"w1_raw{a}{u}")
+                rows = w1[512 * a : 512 * (a + 1), half * u : half * (u + 1)]
+                nc.sync.dma_start(out=raw[:], in_=rows.rearrange("(p t) c -> p t c", t=PACK))
+                w1_raw[a, u] = raw
+        gains = keep.tile([P, PACK], F32, name="gains")
+        nc.sync.dma_start(out=gains[:], in_=gain.rearrange("(p t) -> p t", t=PACK))
+        nc.sync.dma_start(idx2[:], offs2)
+        put_weight = keep.tile([P, S], F32, name="put_weight")
+        nc.sync.dma_start(out=put_weight[:], in_=wgs)
+        nc.sync.dma_start(idx3[:], offs3)
+        get_weight = keep.tile([P, M], F32, name="get_weight")
+        nc.sync.dma_start(out=get_weight[:], in_=wgt)
+        w3_raw = keep.tile([P, PACK, N], F32, name="w3_raw")
+        nc.sync.dma_start(out=w3_raw[:], in_=w3.rearrange("(p t) c -> p t c", t=PACK))
+        w4_codes = keep.tile([P, 2 * N], U8, name="w4_codes", align_bytes=64)
+        nc.sync.dma_start(out=w4_codes[:].bitcast(I32), in_=w4_words[0].bitcast(I32))
+        load_scale_rows(nc.sync, w4_plane, w4_scales, 1)
+        pricking = keep.tile([P, PACK, M], F32, name="pricking")
+        nc.sync.dma_start(out=pricking[:], in_=prick.rearrange("(p t) m -> p t m", t=PACK))
+
+        warm = keep.tile([P, 2], F32, name="warm")
+        nc.vector.memset(warm[:, 0:1], 0.0)
+        nc.scalar.activation(out=warm[:, 1:2], in_=warm[:, 0:1], func=ACT.Sin)
+        ident = keep.tile([P, P], F32, name="ident")
+        make_identity(nc, ident[:])
+        pages = []
+        for t in range(PACK):
+            page = keep.tile([P, T2], F32, name=f"page{t}")
+            nc.gpsimd.memset(page[:], 0.0)
+            pages.append(page)
+
+        picked = {}
+
+        def pick(q):
+            offsets = idx[:, q * PICK // 16 : (q + 1) * PICK // 16]
+            planes, codes = [], []
+            for a in range(PASSES):
+                plane = keep.tile([P, PICK], U8, name=f"picked_plane{q}{a}", align_bytes=64)
+                nc.vector.tensor_copy(plane[:], tab_plane[:, a * T : (a + 1) * T].indirect(offsets))
+                planes.append(plane)
+            for a in range(PASSES):
+                words = keep.tile([P, PICK], U32, name=f"picked_codes{q}{a}", align_bytes=64)
+                nc.vector.tensor_copy(words[:], tab[a][:].bitcast(U32).indirect(offsets))
+                codes.append(words)
+            picked[q] = (codes, planes)
+
+        w1_codes = [keep.tile([P, H], U32, name=f"w1_codes{a}", align_bytes=64) for a in range(PASSES)]
+        w1_plane = [keep.tile([P, H], U8, name=f"w1_plane{a}", align_bytes=64) for a in range(PASSES)]
+
+        def quantise_w1(a, u, copy):
+            grouped = keep.tile([P, half, PACK], BF16, name=f"w1_grouped{a}{u}", align_bytes=64)
+            interleave(copy, grouped[:], w1_raw[a, u][:])
+            cols = slice(half * u, half * (u + 1))
+            nc.vector.quantize_mx(
+                out=w1_codes[a][:, cols].bitcast(FP8X4), scales=w1_plane[a][:, cols],
+                in_=grouped[:].rearrange("p c t -> p (c t)"),
+            )
+
+        def sine(block, moving, shift, sign, result):
+            codes, planes = picked[block * P // PICK]
+            cols = slice(block * P % PICK, block * P % PICK + P)
+            angle = psum.tile([P, H], F32, name="angle", tag="acc", bufs=6)
+            for a in range(PASSES):
+                nc.tensor.matmul_mx(
+                    out=angle[:], lhsT=codes[a][:, cols].bitcast(FP8X4), lhsT_scale=planes[a][:, cols],
+                    rhs=moving[a][0], rhs_scale=moving[a][1], start=(a == 0), stop=(a == PASSES - 1),
+                )
+            dealt = angle[:].rearrange("j (p t) -> j t p", t=PACK)
+            turns = ring.tile([P, PACK, P], F32, name="turns")
+            nc.scalar.activation(out=turns[:], in_=dealt, func=ACT.Abs, scale=1.0 / TURN, bias=shift)
+            whole = ring.tile([P, PACK, P], U32, name="whole")
+            nc.scalar.activation(out=whole[:], in_=turns[:], func=ACT.Copy, scale=1.0, bias=0.25)
+            rest = ring.tile([P, PACK, P], F32, name="rest")
+            nc.vector.scalar_tensor_tensor(
+                out=rest[:], in0=turns[:], scalar=0.25, in1=whole[:].bitcast(I32), op0=ALU.add, op1=ALU.subtract
+            )
+            nc.scalar.activation(out=result[:], in_=rest[:], func=ACT.Sin, scale=sign * TURN)
+
+        w2_moving = [
+            (w2_codes[:, 2 * H * a : 2 * H * (a + 1)].bitcast(FP4X4), w2_plane[:, H * a : H * (a + 1)])
+            for a in range(PASSES)
+        ]
+        w1_moving = [(w1_codes[a][:].bitcast(FP8X4), w1_plane[a][:]) for a in range(PASSES)]
+        minus_sin = {}
+        cosine = {}
+
+        def second_angle(block):
+            minus_sin[block] = keep.tile([P, PACK, P], F32, name=f"minus_sin{block}")
+            sine(block, w2_moving, -0.25, -1.0, minus_sin[block])
+
+        def first_angle(block):
+            cosine[block] = ring.tile([P, PACK, P], F32, name="cosine")
+            sine(block, w1_moving, 0.0, 1.0, cosine[block])
+
+        def put(block):
+            diff = psum.tile([P, PACK, P], F32, name="diff", tag="diff", bufs=2)
+            for t in range(PACK):
+                nc.tensor.matmul(diff[:, t, :], lhsT=cosine[block][:, t, :], rhs=ident[:],
+                                 is_transpose=True, start=True, stop=False)
+                nc.tensor.matmul(diff[:, t, :], lhsT=minus_sin[block][:, t, :], rhs=ident[:],
+                                 is_transpose=True, start=False, stop=True)
+            h = ring.tile([P, PACK, P], F32, name="h")
+            for t in range(PACK):
+                nc.scalar.activation(out=h[:, t, :], in_=diff[:, t, :], func=ACT.Copy, scale=gains[:, t : t + 1])
+            offsets = idx2[:, block * P // 16 : (block + 1) * P // 16]
+            for t in range(PACK):
+                nc.vector.tensor_tensor(
+                    pages[t][:].indirect(offsets), h[:, t, :], put_weight[:, block * P : (block + 1) * P], ALU.mult
+                )
+
+        pick(0)
+        second_angle(0)
+        second_angle(1)
+        pick(1)
+        second_angle(2)
+        quantise_w1(0, 0, nc.scalar.copy)
+        quantise_w1(0, 1, nc.scalar.copy)
+        pick(2)
+        second_angle(3)
+        quantise_w1(1, 0, nc.scalar.copy)
+        quantise_w1(1, 1, nc.vector.tensor_copy)
+        first_angle(0)
+        pick(3)
+        for block in range(BLOCKS):
+            if block + 1 < BLOCKS:
+                first_angle(block + 1)
+            put(block)
+            if block + AHEAD < BLOCKS:
+                second_angle(block + AHEAD)
+
+        w3_grouped = keep.tile([P, N, PACK], BF16, name="w3_grouped", align_bytes=64)
+        interleave(nc.scalar.copy, w3_grouped[:], w3_raw[:])
+        w3_codes = keep.tile([P, N], U32, name="w3_codes", align_bytes=64)
+        w3_plane = keep.tile([P, N], U8, name="w3_plane", align_bytes=64)
+        for cols in (slice(0, 256), slice(256, N)):
+            nc.vector.quantize_mx(
+                out=w3_codes[:, cols].bitcast(FP8X4), scales=w3_plane[:, cols],
+                in_=w3_grouped[:, cols, :].rearrange("p c t -> p (c t)"),
+            )
+
+        out_rows = out.rearrange("(g p) m -> p g m", p=P)
+        grouped_z = {}
+
+        def get(start, width):
+            cols = slice(start, start + width)
+            offsets = idx3[:, start // 16 : (start + width) // 16]
+            x = ring.tile([P, PACK, width], F32, name="x")
+            for t in range(PACK):
+                nc.vector.tensor_tensor(x[:, t, :], pages[t][:].indirect(offsets), get_weight[:, cols], ALU.mult)
+            z = ring.tile([P, PACK, width], BF16, name="z")
+            nc.vector.tensor_tensor(z[:], x[:], pricking[:, :, cols], ALU.subtract)
+            grouped = ring.tile([P, width, PACK], BF16, name="z_grouped", align_bytes=64)
+            interleave(nc.scalar.copy, grouped[:], z[:])
+            grouped_z[start] = grouped
+
+        sums = {}
+
+        def project(start, width):
+            z_codes = ring.tile([P, width], U32, name="z_codes", align_bytes=64)
+            z_plane = ring.tile([P, width], U8, name="z_plane", align_bytes=64)
+            nc.vector.quantize_mx(
+                out=z_codes[:].bitcast(FP8X4), scales=z_plane[:],
+                in_=grouped_z[start][:].rearrange("p c t -> p (c t)"),
+            )
+            per_bank = 512 // width
+            sums[start] = []
+            for first in range(0, N // P, per_bank):
+                count = min(per_bank, N // P - first)
+                y1 = psum.tile([P, count, width], F32, name="y1", tag="acc", bufs=6)
+                y2 = psum.tile([P, count, width], F32, name="y2", tag="acc", bufs=6)
+                for g in range(count):
+                    n0 = (first + g) * P
+                    nc.tensor.matmul_mx(
+                        out=y2[:, g, :], lhsT=w4_codes[:, 2 * n0 : 2 * (n0 + P)].bitcast(FP4X4),
+                        lhsT_scale=w4_plane[:, n0 : n0 + P], rhs=z_codes[:].bitcast(FP8X4), rhs_scale=z_plane[:],
+                        start=True, stop=True,
+                    )
+                for g in range(count):
+                    n0 = (first + g) * P
+                    nc.tensor.matmul_mx(
+                        out=y1[:, g, :], lhsT=w3_codes[:, n0 : n0 + P].bitcast(FP8X4),
+                        lhsT_scale=w3_plane[:, n0 : n0 + P], rhs=z_codes[:].bitcast(FP8X4), rhs_scale=z_plane[:],
+                        start=True, stop=True,
+                    )
+                y2_plus = ring.tile([P, count, width], F32, name="y2_plus", bufs=4)
+                nc.scalar.activation(out=y2_plus[:], in_=y2[:], func=ACT.Copy, scale=1.0, bias=1.0)
+                sums[start].append((first, count, y1, y2_plus))
+
+        def finish(start, width):
+            result = ring.tile([P, N // P, width], F32, name="result")
+            for first, count, y1, y2_plus in sums[start]:
+                nc.vector.tensor_tensor(result[:, first : first + count, :], y1[:], y2_plus[:], ALU.mult)
+            nc.sync.dma_start(out=out_rows[:, :, start : start + width], in_=result[:])
+
+        starts = [sum(CHUNKS[:c]) for c in range(len(CHUNKS))]
+        chunks = list(zip(starts, CHUNKS))
+        for step in range(len(chunks) + 2):
+            if step < len(chunks):
+                get(*chunks[step])
+            if 0 <= step - 1 < len(chunks):
+                project(*chunks[step - 1])
+            if 0 <= step - 2 < len(chunks):
+                finish(*chunks[step - 2])

@@ -21,11 +21,9 @@ ACT = mybir.ActivationFunctionType
 P = 128
 PACK = 4
 PASSES = K // (P * PACK)
-PICK = 256
 BLOCKS = S // P
 TURN = 2.0 * math.pi
 CHUNKS = (256, 256, 256, 128, 128)
-AHEAD = 4
 
 
 def tile_list_bobbin_path_features_kernel(
@@ -58,157 +56,214 @@ def tile_list_bobbin_path_features_kernel(
         idx3 = lists.tile([P, M // 16], U16, name="idx3")
 
         tab_plane = keep.tile([P, PASSES * T], U8, name="tab_plane", align_bytes=64)
-        w2_plane = keep.tile([P, PASSES * H], U8, name="w2_plane", align_bytes=64)
-        w4_plane = keep.tile([P, N], U8, name="w4_plane", align_bytes=64)
-        for plane in (tab_plane, w2_plane, w4_plane):
-            nc.vector.memset(plane[:].bitcast(I32), 0)
-
+        nc.vector.memset(tab_plane[:].bitcast(I32), 0)
         nc.sync.dma_start(idx[:], offs)
-        load_scale_rows(nc.scalar, tab_plane, tab_scales, PASSES)
-        tab = []
-        for a in range(PASSES):
-            words = keep.tile([P, T], I32, name=f"tab{a}", align_bytes=64)
-            nc.sync.dma_start(out=words[:], in_=tab_words[a].rearrange("p t i -> p (t i)").bitcast(I32))
-            tab.append(words)
-        w2_codes = keep.tile([P, PASSES * 2 * H], U8, name="w2_codes", align_bytes=64)
+        load_scale_rows(nc.sync, tab_plane, tab_scales, PASSES)
+        shared = ctx.enter_context(tc.tile_pool(name="shared", bufs=1))
+        with tc.tile_pool(name="first", bufs=1) as first_pool:
+            warm = first_pool.tile([P, 2], F32, name="warm")
+            nc.vector.memset(warm[:, 0:1], 0.0)
+            nc.scalar.activation(out=warm[:, 1:2], in_=warm[:, 0:1], func=ACT.Sin)
+        late = ctx.enter_context(tc.tile_pool(name="late", bufs=1))
+
+        half = H // 2
+        tab, w1_raw = {}, {}
+
+        def load_table(a, pool):
+            tab[a] = pool.tile([P, T], I32, name=f"tab{a}", align_bytes=64)
+            nc.sync.dma_start(out=tab[a][:], in_=tab_words[a].rearrange("p t i -> p (t i)").bitcast(I32))
+
+        def load_w1(a, start, stop, pool):
+            w1_raw[a, start] = pool.tile([P, PACK, stop - start], F32, name=f"w1_raw{a}{start}")
+            rows = w1[512 * a : 512 * (a + 1), start:stop]
+            nc.sync.dma_start(out=w1_raw[a, start][:], in_=rows.rearrange("(p t) c -> p t c", t=PACK))
+
+        load_table(0, keep)
+        load_table(1, late)
+        w2_codes = late.tile([P, PASSES * 2 * H], U8, name="w2_codes", align_bytes=64)
         nc.sync.dma_start(
             out=w2_codes[:].bitcast(I32).rearrange("p (a n) -> p a n", a=PASSES),
             in_=w2_words.bitcast(I32).rearrange("a p n -> p a n"),
         )
-        load_scale_rows(nc.scalar, w2_plane, w2_scales, PASSES)
-        half = H // 2
-        w1_raw = {}
-        for a in range(PASSES):
-            for u in range(2):
-                raw = keep.tile([P, PACK, half], F32, name=f"w1_raw{a}{u}")
-                rows = w1[512 * a : 512 * (a + 1), half * u : half * (u + 1)]
-                nc.sync.dma_start(out=raw[:], in_=rows.rearrange("(p t) c -> p t c", t=PACK))
-                w1_raw[a, u] = raw
-        gains = keep.tile([P, PACK], F32, name="gains")
+        w2_plane = late.tile([P, PASSES * H], U8, name="w2_plane", align_bytes=64)
+        nc.vector.memset(w2_plane[:].bitcast(I32), 0)
+        load_scale_rows(nc.sync, w2_plane, w2_scales, PASSES)
+        load_w1(0, 0, H, late)
+        load_w1(1, 0, half, late)
+        load_w1(1, half, H, late)
+        gains = late.tile([P, PACK], F32, name="gains")
         nc.sync.dma_start(out=gains[:], in_=gain.rearrange("(p t) -> p t", t=PACK))
         nc.sync.dma_start(idx2[:], offs2)
-        put_weight = keep.tile([P, S], F32, name="put_weight")
+        put_weight = late.tile([P, S], F32, name="put_weight")
         nc.sync.dma_start(out=put_weight[:], in_=wgs)
         nc.sync.dma_start(idx3[:], offs3)
-        get_weight = keep.tile([P, M], F32, name="get_weight")
+        get_weight = late.tile([P, M], F32, name="get_weight")
         nc.sync.dma_start(out=get_weight[:], in_=wgt)
-        w3_raw = keep.tile([P, PACK, N], F32, name="w3_raw")
+        w3_raw = late.tile([P, PACK, N], F32, name="w3_raw")
         nc.sync.dma_start(out=w3_raw[:], in_=w3.rearrange("(p t) c -> p t c", t=PACK))
-        w4_codes = keep.tile([P, 2 * N], U8, name="w4_codes", align_bytes=64)
+        w4_codes = late.tile([P, 2 * N], U8, name="w4_codes", align_bytes=64)
         nc.sync.dma_start(out=w4_codes[:].bitcast(I32), in_=w4_words[0].bitcast(I32))
+        w4_plane = late.tile([P, N], U8, name="w4_plane", align_bytes=64)
+        nc.vector.memset(w4_plane[:].bitcast(I32), 0)
         load_scale_rows(nc.sync, w4_plane, w4_scales, 1)
-        pricking = keep.tile([P, PACK, M], F32, name="pricking")
+        pricking = late.tile([P, PACK, M], F32, name="pricking")
         nc.sync.dma_start(out=pricking[:], in_=prick.rearrange("(p t) m -> p t m", t=PACK))
 
-        warm = keep.tile([P, 2], F32, name="warm")
-        nc.vector.memset(warm[:, 0:1], 0.0)
-        nc.scalar.activation(out=warm[:, 1:2], in_=warm[:, 0:1], func=ACT.Sin)
         ident = keep.tile([P, P], F32, name="ident")
         make_identity(nc, ident[:])
         pages = []
         for t in range(PACK):
             page = keep.tile([P, T2], F32, name=f"page{t}")
-            nc.gpsimd.memset(page[:], 0.0)
+            nc.vector.memset(page[:], 0.0)
             pages.append(page)
 
+        early = 2 * P
         picked = {}
 
-        def pick(q):
-            offsets = idx[:, q * PICK // 16 : (q + 1) * PICK // 16]
-            planes, codes = [], []
+        def pick(a, start, stop, pool, **place):
+            words = pool.tile([P, stop - start], U32, name=f"picked{a}{start}", align_bytes=64, **place)
+            nc.vector.tensor_copy(words[:], tab[a][:].bitcast(U32).indirect(idx[:, start // 16 : stop // 16]))
+            for block in range(start // P, stop // P):
+                picked[a, block] = words[:, block * P - start : (block + 1) * P - start]
+
+        picked_planes = {}
+
+        def pick_scales(start, stop, pool, **place):
+            planes = pool.tile([P, PASSES, stop - start], U8, name=f"picked_planes{start}", align_bytes=64, **place)
             for a in range(PASSES):
-                plane = keep.tile([P, PICK], U8, name=f"picked_plane{q}{a}", align_bytes=64)
-                nc.vector.tensor_copy(plane[:], tab_plane[:, a * T : (a + 1) * T].indirect(offsets))
-                planes.append(plane)
-            for a in range(PASSES):
-                words = keep.tile([P, PICK], U32, name=f"picked_codes{q}{a}", align_bytes=64)
-                nc.vector.tensor_copy(words[:], tab[a][:].bitcast(U32).indirect(offsets))
-                codes.append(words)
-            picked[q] = (codes, planes)
+                window = tab_plane[:, a * T : (a + 1) * T]
+                nc.vector.tensor_copy(planes[:, a, :], window.indirect(idx[:, start // 16 : stop // 16]))
+                for block in range(start // P, stop // P):
+                    picked_planes[a, block] = planes[:, a, block * P - start : (block + 1) * P - start]
 
         w1_codes = [keep.tile([P, H], U32, name=f"w1_codes{a}", align_bytes=64) for a in range(PASSES)]
         w1_plane = [keep.tile([P, H], U8, name=f"w1_plane{a}", align_bytes=64) for a in range(PASSES)]
 
-        def quantise_w1(a, u, copy):
-            grouped = keep.tile([P, half, PACK], BF16, name=f"w1_grouped{a}{u}", align_bytes=64)
-            interleave(copy, grouped[:], w1_raw[a, u][:])
-            cols = slice(half * u, half * (u + 1))
-            nc.vector.quantize_mx(
-                out=w1_codes[a][:, cols].bitcast(FP8X4), scales=w1_plane[a][:, cols],
-                in_=grouped[:].rearrange("p c t -> p (c t)"),
+        w1_grouped = [
+            keep.tile([P, PACK, P, PACK], BF16, name="w1_grouped0", align_bytes=64),
+            shared.tile([P, PACK, P, PACK], BF16, name="w1_grouped1", align_bytes=64, offset=0),
+        ]
+
+        def deal_w1(a, start, stop, copy):
+            copy(
+                out=w1_grouped[a][:, :, start // PACK : stop // PACK, :].rearrange("p t m i -> p m i t"),
+                in_=w1_raw[a, start][:].rearrange("p i (m t) -> p m i t", t=PACK),
             )
 
-        def sine(block, moving, shift, sign, result):
-            codes, planes = picked[block * P // PICK]
-            cols = slice(block * P % PICK, block * P % PICK + P)
-            angle = psum.tile([P, H], F32, name="angle", tag="acc", bufs=6)
-            for a in range(PASSES):
-                nc.tensor.matmul_mx(
-                    out=angle[:], lhsT=codes[a][:, cols].bitcast(FP8X4), lhsT_scale=planes[a][:, cols],
-                    rhs=moving[a][0], rhs_scale=moving[a][1], start=(a == 0), stop=(a == PASSES - 1),
-                )
-            dealt = angle[:].rearrange("j (p t) -> j t p", t=PACK)
-            turns = ring.tile([P, PACK, P], F32, name="turns")
-            nc.scalar.activation(out=turns[:], in_=dealt, func=ACT.Abs, scale=1.0 / TURN, bias=shift)
-            whole = ring.tile([P, PACK, P], U32, name="whole")
-            nc.scalar.activation(out=whole[:], in_=turns[:], func=ACT.Copy, scale=1.0, bias=0.25)
-            rest = ring.tile([P, PACK, P], F32, name="rest")
-            nc.vector.scalar_tensor_tensor(
-                out=rest[:], in0=turns[:], scalar=0.25, in1=whole[:].bitcast(I32), op0=ALU.add, op1=ALU.subtract
+        def quantise_w1(a):
+            nc.vector.quantize_mx(
+                out=w1_codes[a][:].bitcast(FP8X4), scales=w1_plane[a][:],
+                in_=w1_grouped[a][:].rearrange("p t m i -> p (t m i)"),
             )
-            nc.scalar.activation(out=result[:], in_=rest[:], func=ACT.Sin, scale=sign * TURN)
 
         w2_moving = [
             (w2_codes[:, 2 * H * a : 2 * H * (a + 1)].bitcast(FP4X4), w2_plane[:, H * a : H * (a + 1)])
             for a in range(PASSES)
         ]
         w1_moving = [(w1_codes[a][:].bitcast(FP8X4), w1_plane[a][:]) for a in range(PASSES)]
-        minus_sin = {}
-        cosine = {}
+        COS, SIN = 0, 1
+        moving = (w1_moving, w2_moving)
+        shift = (0.0, 0.25)
+        groups = [(0,), (1,), (2, 3), (4, 5), (6, 7)]
+        waves = [
+            keep.tile([P, 2, len(blocks), PACK, P], F32, name=f"wave{g}") for g, blocks in enumerate(groups)
+        ]
+        wholes = [
+            ring.tile([P, 2, len(blocks), PACK, P], I32, name="whole", bufs=2) for g, blocks in enumerate(groups)
+        ]
 
-        def second_angle(block):
-            minus_sin[block] = keep.tile([P, PACK, P], F32, name=f"minus_sin{block}")
-            sine(block, w2_moving, -0.25, -1.0, minus_sin[block])
+        def flat(tile):
+            return tile[:].rearrange("j k b t p -> j (k b t p)")
 
-        def first_angle(block):
-            cosine[block] = ring.tile([P, PACK, P], F32, name="cosine")
-            sine(block, w1_moving, 0.0, 1.0, cosine[block])
+        def turns(g, kind, parts):
+            for b, block in enumerate(groups[g]):
+                angle = psum.tile([P, H], F32, name="angle", tag="product", bufs=4)
+                for a in range(PASSES):
+                    nc.tensor.matmul_mx(
+                        out=angle[:], lhsT=picked[a, block].bitcast(FP8X4), lhsT_scale=picked_planes[a, block],
+                        rhs=moving[kind][a][0], rhs_scale=moving[kind][a][1], start=(a == 0), stop=(a == PASSES - 1),
+                    )
+                if kind == COS:
+                    steps = [
+                        (waves[g][:, kind, b, ts, :], angle[:].rearrange("j (t p) -> j t p", t=PACK)[:, ts, :])
+                        for ts in parts
+                    ]
+                else:
+                    steps = [
+                        (waves[g][:, kind, b].rearrange("j t p -> j p t"), angle[:].rearrange("j (p t) -> j p t", t=PACK))
+                    ]
+                for into, source in steps:
+                    nc.scalar.activation(out=into, in_=source, func=ACT.Abs, scale=1.0 / TURN, bias=shift[kind])
 
-        def put(block):
-            diff = psum.tile([P, PACK, P], F32, name="diff", tag="diff", bufs=2)
-            for t in range(PACK):
-                nc.tensor.matmul(diff[:, t, :], lhsT=cosine[block][:, t, :], rhs=ident[:],
-                                 is_transpose=True, start=True, stop=False)
-                nc.tensor.matmul(diff[:, t, :], lhsT=minus_sin[block][:, t, :], rhs=ident[:],
-                                 is_transpose=True, start=False, stop=True)
-            h = ring.tile([P, PACK, P], F32, name="h")
-            for t in range(PACK):
-                nc.scalar.activation(out=h[:, t, :], in_=diff[:, t, :], func=ACT.Copy, scale=gains[:, t : t + 1])
-            offsets = idx2[:, block * P // 16 : (block + 1) * P // 16]
+        def round_on_scalar(wave, whole):
+            nc.scalar.activation(out=whole.bitcast(U32), in_=wave, func=ACT.Copy, scale=1.0, bias=0.25)
+
+        def round_on_vector(wave, whole):
+            nc.vector.tensor_scalar(out=whole, in0=wave, scalar1=0.25, scalar2=None, op0=ALU.add)
+
+        def rest(wave, whole):
+            nc.vector.scalar_tensor_tensor(out=wave, in0=wave, scalar=0.25, in1=whole, op0=ALU.add, op1=ALU.subtract)
+
+        def sine(wave):
+            nc.scalar.activation(out=wave, in_=wave, func=ACT.Sin, scale=TURN)
+
+        def put(g, per_bank):
+            blocks = groups[g]
+            width = len(blocks) * P
+            start = blocks[0] * P
+            h = ring.tile([P, PACK, width], F32, name="h")
+            for t0 in range(0, PACK, per_bank):
+                diff = psum.tile([P, per_bank, width], F32, name="diff", tag="sum", bufs=4)
+                for t in range(t0, t0 + per_bank):
+                    for b in range(len(blocks)):
+                        for kind in (SIN, COS):
+                            nc.tensor.matmul(diff[:, t - t0, b * P : (b + 1) * P], lhsT=waves[g][:, kind, b, t, :],
+                                             rhs=ident[:], is_transpose=True, start=(kind == SIN), stop=(kind == COS))
+                for t in range(t0, t0 + per_bank):
+                    nc.scalar.activation(out=h[:, t, :], in_=diff[:, t - t0, :], func=ACT.Copy, scale=gains[:, t : t + 1])
+            offsets = idx2[:, start // 16 : (start + width) // 16]
             for t in range(PACK):
                 nc.vector.tensor_tensor(
-                    pages[t][:].indirect(offsets), h[:, t, :], put_weight[:, block * P : (block + 1) * P], ALU.mult
+                    pages[t][:].indirect(offsets), h[:, t, :], put_weight[:, start : start + width], ALU.mult
                 )
 
-        pick(0)
-        second_angle(0)
-        second_angle(1)
-        pick(1)
-        second_angle(2)
-        quantise_w1(0, 0, nc.scalar.copy)
-        quantise_w1(0, 1, nc.scalar.copy)
-        pick(2)
-        second_angle(3)
-        quantise_w1(1, 0, nc.scalar.copy)
-        quantise_w1(1, 1, nc.vector.tensor_copy)
-        first_angle(0)
-        pick(3)
-        for block in range(BLOCKS):
-            if block + 1 < BLOCKS:
-                first_angle(block + 1)
-            put(block)
-            if block + AHEAD < BLOCKS:
-                second_angle(block + AHEAD)
+        at_once = [slice(0, PACK)]
+        one_by_one = [slice(t, t + 1) for t in range(PACK)]
+        pick(0, 0, S, keep)
+        pick_scales(0, S // 2, keep)
+        pick(1, 0, early, keep)
+        turns(0, SIN, at_once)
+        pick(1, early, S, keep)
+        deal_w1(0, 0, H, nc.scalar.copy)
+        quantise_w1(0)
+        deal_w1(1, 0, half, nc.scalar.copy)
+        deal_w1(1, half, H, nc.vector.tensor_copy)
+        quantise_w1(1)
+        round_on_vector(waves[0][:, SIN, 0], wholes[0][:, SIN, 0])
+        rest(waves[0][:, SIN, 0], wholes[0][:, SIN, 0])
+        sine(waves[0][:, SIN, 0])
+        turns(0, COS, one_by_one)
+        for t in range(PACK):
+            round_on_vector(waves[0][:, COS, 0, t], wholes[0][:, COS, 0, t])
+        for t in range(PACK):
+            rest(waves[0][:, COS, 0, t], wholes[0][:, COS, 0, t])
+            sine(waves[0][:, COS, 0, t])
+        turns(1, SIN, at_once)
+        turns(1, COS, at_once)
+        round_on_vector(flat(waves[1]), flat(wholes[1]))
+        rest(flat(waves[1]), flat(wholes[1]))
+        put(0, 1)
+        pick_scales(S // 2, S, shared, offset=0)
+        for g in range(1, len(groups)):
+            ahead = g + 1 < len(groups)
+            if ahead:
+                turns(g + 1, SIN, at_once)
+                turns(g + 1, COS, at_once)
+            sine(flat(waves[g]))
+            if ahead:
+                round_on_scalar(flat(waves[g + 1]), flat(wholes[g + 1]))
+                rest(flat(waves[g + 1]), flat(wholes[g + 1]))
+            put(g, 512 // (len(groups[g]) * P))
 
         w3_grouped = keep.tile([P, N, PACK], BF16, name="w3_grouped", align_bytes=64)
         interleave(nc.scalar.copy, w3_grouped[:], w3_raw[:])
@@ -223,16 +278,17 @@ def tile_list_bobbin_path_features_kernel(
         out_rows = out.rearrange("(g p) m -> p g m", p=P)
         grouped_z = {}
 
-        def get(start, width):
-            cols = slice(start, start + width)
+        def get(start, width, copy):
             offsets = idx3[:, start // 16 : (start + width) // 16]
-            x = ring.tile([P, PACK, width], F32, name="x")
+            x = ring.tile([P, PACK, width], F32, name="x", tag="x_or_z", align_bytes=64)
             for t in range(PACK):
-                nc.vector.tensor_tensor(x[:, t, :], pages[t][:].indirect(offsets), get_weight[:, cols], ALU.mult)
+                nc.vector.tensor_tensor(
+                    x[:, t, :], pages[t][:].indirect(offsets), get_weight[:, start : start + width], ALU.mult
+                )
             z = ring.tile([P, PACK, width], BF16, name="z")
-            nc.vector.tensor_tensor(z[:], x[:], pricking[:, :, cols], ALU.subtract)
-            grouped = ring.tile([P, width, PACK], BF16, name="z_grouped", align_bytes=64)
-            interleave(nc.scalar.copy, grouped[:], z[:])
+            nc.vector.tensor_tensor(z[:], x[:], pricking[:, :, start : start + width], ALU.subtract)
+            grouped = ring.tile([P, width, PACK], BF16, name="z_grouped", tag="x_or_z", align_bytes=64)
+            interleave(copy, grouped[:], z[:])
             grouped_z[start] = grouped
 
         sums = {}
@@ -248,8 +304,8 @@ def tile_list_bobbin_path_features_kernel(
             sums[start] = []
             for first in range(0, N // P, per_bank):
                 count = min(per_bank, N // P - first)
-                y1 = psum.tile([P, count, width], F32, name="y1", tag="acc", bufs=6)
-                y2 = psum.tile([P, count, width], F32, name="y2", tag="acc", bufs=6)
+                y1 = psum.tile([P, count, width], F32, name="y1", tag="product", bufs=4)
+                y2 = psum.tile([P, count, width], F32, name="y2", tag="sum", bufs=4)
                 for g in range(count):
                     n0 = (first + g) * P
                     nc.tensor.matmul_mx(
@@ -278,7 +334,7 @@ def tile_list_bobbin_path_features_kernel(
         chunks = list(zip(starts, CHUNKS))
         for step in range(len(chunks) + 2):
             if step < len(chunks):
-                get(*chunks[step])
+                get(*chunks[step], nc.scalar.copy if step + 1 < len(chunks) else nc.vector.tensor_copy)
             if 0 <= step - 1 < len(chunks):
                 project(*chunks[step - 1])
             if 0 <= step - 2 < len(chunks):

import math
from contextlib import ExitStack

import concourse.mybir as mybir
from concourse.masks import make_identity

K, T, S, M, T2, H, N = 1024, 2048, 1024, 1024, 2048, 512, 384
FLOPS = 2 * 2 * K * H * S + 2 * 2 * H * N * M

F32 = mybir.dt.float32
BF16 = mybir.dt.bfloat16
I32 = mybir.dt.int32
U32 = mybir.dt.uint32
U16 = mybir.dt.uint16
U8 = mybir.dt.uint8
FP8X4 = mybir.dt.float8_e4m3fn_x4
FP4X4 = mybir.dt.float4_e2m1fn_x4
ALU = mybir.AluOpType
ACT = mybir.ActivationFunctionType

P = 128
PACK = 4
PASSES = K // (P * PACK)
BLOCKS = S // P
TURN = 2.0 * math.pi
CHUNKS = (256, 256, 256, 128, 128)


def tile_list_bobbin_path_features_kernel(
    tc, tab_words, tab_scales, w1, w2_words, w2_scales, gain, wgs, wgt, prick,
    w3, w4_words, w4_scales, offs, offs2, offs3, out,
):
    nc = tc.nc
    with ExitStack() as ctx:
        lists = ctx.enter_context(tc.tile_pool(name="lists", bufs=1))
        keep = ctx.enter_context(tc.tile_pool(name="keep", bufs=1))
        ring = ctx.enter_context(tc.tile_pool(name="ring", bufs=3))
        psum = ctx.enter_context(tc.psum_pool(name="psum", bufs=1))

        def load_scale_rows(queue, plane, rows, passes):
            words = rows.bitcast(I32)
            for quad in range(4):
                queue.dma_start(
                    out=plane[32 * quad : 32 * quad + 4, :].bitcast(I32).rearrange("r (a n) -> r a n", a=passes),
                    in_=words[:, 4 * quad : 4 * quad + 4, :].rearrange("a r n -> r a n"),
                )

        def interleave(copy, grouped, planes):
            copy(
                out=grouped.rearrange("p (c i) t -> p c t i", i=4),
                in_=planes.rearrange("p t (c i) -> p c t i", i=4),
            )

        idx = lists.tile([P, S // 16], U16, name="idx")
        idx2 = lists.tile([P, S // 16], U16, name="idx2")
        idx3 = lists.tile([P, M // 16], U16, name="idx3")

        tab_plane = keep.tile([P, PASSES * T], U8, name="tab_plane", align_bytes=64)
        nc.vector.memset(tab_plane[:].bitcast(I32), 0)
        nc.sync.dma_start(idx[:], offs)
        load_scale_rows(nc.sync, tab_plane, tab_scales, PASSES)
        shared = ctx.enter_context(tc.tile_pool(name="shared", bufs=1))
        with tc.tile_pool(name="first", bufs=1) as first_pool:
            warm = first_pool.tile([P, 2], F32, name="warm")
            nc.vector.memset(warm[:, 0:1], 0.0)
            nc.scalar.activation(out=warm[:, 1:2], in_=warm[:, 0:1], func=ACT.Sin)
        late = ctx.enter_context(tc.tile_pool(name="late", bufs=1))

        half = H // 2
        tab, w1_raw = {}, {}

        def load_table(a, pool):
            tab[a] = pool.tile([P, T], I32, name=f"tab{a}", align_bytes=64)
            nc.sync.dma_start(out=tab[a][:], in_=tab_words[a].rearrange("p t i -> p (t i)").bitcast(I32))

        def load_w1(a, start, stop, pool):
            w1_raw[a, start] = pool.tile([P, PACK, stop - start], F32, name=f"w1_raw{a}{start}")
            rows = w1[512 * a : 512 * (a + 1), start:stop]
            nc.sync.dma_start(out=w1_raw[a, start][:], in_=rows.rearrange("(p t) c -> p t c", t=PACK))

        load_table(0, keep)
        load_table(1, late)
        w2_codes = late.tile([P, PASSES * 2 * H], U8, name="w2_codes", align_bytes=64)
        nc.sync.dma_start(
            out=w2_codes[:].bitcast(I32).rearrange("p (a n) -> p a n", a=PASSES),
            in_=w2_words.bitcast(I32).rearrange("a p n -> p a n"),
        )
        w2_plane = late.tile([P, PASSES * H], U8, name="w2_plane", align_bytes=64)
        nc.vector.memset(w2_plane[:].bitcast(I32), 0)
        load_scale_rows(nc.sync, w2_plane, w2_scales, PASSES)
        load_w1(0, 0, H, late)
        load_w1(1, 0, half, late)
        load_w1(1, half, H, late)
        gains = late.tile([P, PACK], F32, name="gains")
        nc.sync.dma_start(out=gains[:], in_=gain.rearrange("(p t) -> p t", t=PACK))
        nc.sync.dma_start(idx2[:], offs2)
        put_weight = late.tile([P, S], F32, name="put_weight")
        nc.sync.dma_start(out=put_weight[:], in_=wgs)
        nc.sync.dma_start(idx3[:], offs3)
        get_weight = late.tile([P, M], F32, name="get_weight")
        nc.sync.dma_start(out=get_weight[:], in_=wgt)
        w3_raw = late.tile([P, PACK, N], F32, name="w3_raw")
        nc.sync.dma_start(out=w3_raw[:], in_=w3.rearrange("(p t) c -> p t c", t=PACK))
        w4_codes = late.tile([P, 2 * N], U8, name="w4_codes", align_bytes=64)
        nc.sync.dma_start(out=w4_codes[:].bitcast(I32), in_=w4_words[0].bitcast(I32))
        w4_plane = late.tile([P, N], U8, name="w4_plane", align_bytes=64)
        nc.vector.memset(w4_plane[:].bitcast(I32), 0)
        load_scale_rows(nc.sync, w4_plane, w4_scales, 1)
        pricking = late.tile([P, PACK, M], F32, name="pricking")
        nc.sync.dma_start(out=pricking[:], in_=prick.rearrange("(p t) m -> p t m", t=PACK))

        ident = keep.tile([P, P], F32, name="ident")
        make_identity(nc, ident[:])
        pages = []
        for t in range(PACK):
            page = keep.tile([P, T2], F32, name=f"page{t}")
            nc.vector.memset(page[:], 0.0)
            pages.append(page)

        early = 2 * P
        picked = {}

        def pick(a, start, stop, pool, **place):
            words = pool.tile([P, stop - start], U32, name=f"picked{a}{start}", align_bytes=64, **place)
            nc.vector.tensor_copy(words[:], tab[a][:].bitcast(U32).indirect(idx[:, start // 16 : stop // 16]))
            for block in range(start // P, stop // P):
                picked[a, block] = words[:, block * P - start : (block + 1) * P - start]

        picked_planes = {}

        def pick_scales(start, stop, pool, **place):
            planes = pool.tile([P, PASSES, stop - start], U8, name=f"picked_planes{start}", align_bytes=64, **place)
            for a in range(PASSES):
                window = tab_plane[:, a * T : (a + 1) * T]
                nc.vector.tensor_copy(planes[:, a, :], window.indirect(idx[:, start // 16 : stop // 16]))
                for block in range(start // P, stop // P):
                    picked_planes[a, block] = planes[:, a, block * P - start : (block + 1) * P - start]

        w1_codes = [keep.tile([P, H], U32, name=f"w1_codes{a}", align_bytes=64) for a in range(PASSES)]
        w1_plane = [keep.tile([P, H], U8, name=f"w1_plane{a}", align_bytes=64) for a in range(PASSES)]

        w1_grouped = [
            keep.tile([P, PACK, P, PACK], BF16, name="w1_grouped0", align_bytes=64),
            shared.tile([P, PACK, P, PACK], BF16, name="w1_grouped1", align_bytes=64, offset=0),
        ]

        def deal_w1(a, start, stop, copy):
            copy(
                out=w1_grouped[a][:, :, start // PACK : stop // PACK, :].rearrange("p t m i -> p m i t"),
                in_=w1_raw[a, start][:].rearrange("p i (m t) -> p m i t", t=PACK),
            )

        def quantise_w1(a):
            nc.vector.quantize_mx(
                out=w1_codes[a][:].bitcast(FP8X4), scales=w1_plane[a][:],
                in_=w1_grouped[a][:].rearrange("p t m i -> p (t m i)"),
            )

        w2_moving = [
            (w2_codes[:, 2 * H * a : 2 * H * (a + 1)].bitcast(FP4X4), w2_plane[:, H * a : H * (a + 1)])
            for a in range(PASSES)
        ]
        w1_moving = [(w1_codes[a][:].bitcast(FP8X4), w1_plane[a][:]) for a in range(PASSES)]
        COS, SIN = 0, 1
        moving = (w1_moving, w2_moving)
        shift = (0.0, 0.25)
        groups = [(0,), (1,), (2, 3), (4, 5), (6, 7)]
        waves = [
            keep.tile([P, 2, len(blocks), PACK, P], F32, name=f"wave{g}") for g, blocks in enumerate(groups)
        ]
        wholes = [
            ring.tile([P, 2, len(blocks), PACK, P], I32, name="whole", bufs=2) for g, blocks in enumerate(groups)
        ]

        def flat(tile):
            return tile[:].rearrange("j k b t p -> j (k b t p)")

        def turns(g, kind, parts):
            for b, block in enumerate(groups[g]):
                angle = psum.tile([P, H], F32, name="angle", tag="product", bufs=4)
                for a in range(PASSES):
                    nc.tensor.matmul_mx(
                        out=angle[:], lhsT=picked[a, block].bitcast(FP8X4), lhsT_scale=picked_planes[a, block],
                        rhs=moving[kind][a][0], rhs_scale=moving[kind][a][1], start=(a == 0), stop=(a == PASSES - 1),
                    )
                if kind == COS:
                    steps = [
                        (waves[g][:, kind, b, ts, :], angle[:].rearrange("j (t p) -> j t p", t=PACK)[:, ts, :])
                        for ts in parts
                    ]
                else:
                    steps = [
                        (waves[g][:, kind, b].rearrange("j t p -> j p t"), angle[:].rearrange("j (p t) -> j p t", t=PACK))
                    ]
                for into, source in steps:
                    nc.scalar.activation(out=into, in_=source, func=ACT.Abs, scale=1.0 / TURN, bias=shift[kind])

        def round_on_scalar(wave, whole):
            nc.scalar.activation(out=whole.bitcast(U32), in_=wave, func=ACT.Copy, scale=1.0, bias=0.25)

        def round_on_vector(wave, whole):
            nc.vector.tensor_scalar(out=whole, in0=wave, scalar1=0.25, scalar2=None, op0=ALU.add)

        def rest(wave, whole):
            nc.vector.scalar_tensor_tensor(out=wave, in0=wave, scalar=0.25, in1=whole, op0=ALU.add, op1=ALU.subtract)

        def sine(wave):
            nc.scalar.activation(out=wave, in_=wave, func=ACT.Sin, scale=TURN)

        def put(g, per_bank):
            blocks = groups[g]
            width = len(blocks) * P
            start = blocks[0] * P
            h = ring.tile([P, PACK, width], F32, name="h")
            for t0 in range(0, PACK, per_bank):
                diff = psum.tile([P, per_bank, width], F32, name="diff", tag="sum", bufs=4)
                for t in range(t0, t0 + per_bank):
                    for b in range(len(blocks)):
                        for kind in (SIN, COS):
                            nc.tensor.matmul(diff[:, t - t0, b * P : (b + 1) * P], lhsT=waves[g][:, kind, b, t, :],
                                             rhs=ident[:], is_transpose=True, start=(kind == SIN), stop=(kind == COS))
                for t in range(t0, t0 + per_bank):
                    nc.scalar.activation(out=h[:, t, :], in_=diff[:, t - t0, :], func=ACT.Copy, scale=gains[:, t : t + 1])
            offsets = idx2[:, start // 16 : (start + width) // 16]
            for t in range(PACK):
                nc.vector.tensor_tensor(
                    pages[t][:].indirect(offsets), h[:, t, :], put_weight[:, start : start + width], ALU.mult
                )

        at_once = [slice(0, PACK)]
        one_by_one = [slice(t, t + 1) for t in range(PACK)]
        pick(0, 0, S, keep)
        pick_scales(0, S // 2, keep)
        pick(1, 0, early, keep)
        turns(0, SIN, at_once)
        pick(1, early, S, keep)
        deal_w1(0, 0, H, nc.scalar.copy)
        quantise_w1(0)
        deal_w1(1, 0, half, nc.scalar.copy)
        deal_w1(1, half, H, nc.vector.tensor_copy)
        quantise_w1(1)
        round_on_vector(waves[0][:, SIN, 0], wholes[0][:, SIN, 0])
        rest(waves[0][:, SIN, 0], wholes[0][:, SIN, 0])
        sine(waves[0][:, SIN, 0])
        turns(0, COS, one_by_one)
        for t in range(PACK):
            round_on_vector(waves[0][:, COS, 0, t], wholes[0][:, COS, 0, t])
        for t in range(PACK):
            rest(waves[0][:, COS, 0, t], wholes[0][:, COS, 0, t])
            sine(waves[0][:, COS, 0, t])
        turns(1, SIN, at_once)
        turns(1, COS, at_once)
        round_on_vector(flat(waves[1]), flat(wholes[1]))
        rest(flat(waves[1]), flat(wholes[1]))
        put(0, 1)
        pick_scales(S // 2, S, shared, offset=0)
        for g in range(1, len(groups)):
            ahead = g + 1 < len(groups)
            if ahead:
                turns(g + 1, SIN, at_once)
                turns(g + 1, COS, at_once)
            sine(flat(waves[g]))
            if ahead:
                round_on_scalar(flat(waves[g + 1]), flat(wholes[g + 1]))
                rest(flat(waves[g + 1]), flat(wholes[g + 1]))
            put(g, 512 // (len(groups[g]) * P))

        w3_grouped = keep.tile([P, N, PACK], BF16, name="w3_grouped", align_bytes=64)
        interleave(nc.scalar.copy, w3_grouped[:], w3_raw[:])
        w3_codes = keep.tile([P, N], U32, name="w3_codes", align_bytes=64)
        w3_plane = keep.tile([P, N], U8, name="w3_plane", align_bytes=64)
        for cols in (slice(0, 256), slice(256, N)):
            nc.vector.quantize_mx(
                out=w3_codes[:, cols].bitcast(FP8X4), scales=w3_plane[:, cols],
                in_=w3_grouped[:, cols, :].rearrange("p c t -> p (c t)"),
            )

        out_rows = out.rearrange("(g p) m -> p g m", p=P)
        grouped_z = {}

        def get(start, width, copy):
            offsets = idx3[:, start // 16 : (start + width) // 16]
            x = ring.tile([P, PACK, width], F32, name="x", tag="x_or_z", align_bytes=64)
            for t in range(PACK):
                nc.vector.tensor_tensor(
                    x[:, t, :], pages[t][:].indirect(offsets), get_weight[:, start : start + width], ALU.mult
                )
            z = ring.tile([P, PACK, width], BF16, name="z")
            nc.vector.tensor_tensor(z[:], x[:], pricking[:, :, start : start + width], ALU.subtract)
            grouped = ring.tile([P, width, PACK], BF16, name="z_grouped", tag="x_or_z", align_bytes=64)
            interleave(copy, grouped[:], z[:])
            grouped_z[start] = grouped

        sums = {}

        def project(start, width):
            z_codes = ring.tile([P, width], U32, name="z_codes", align_bytes=64)
            z_plane = ring.tile([P, width], U8, name="z_plane", align_bytes=64)
            nc.vector.quantize_mx(
                out=z_codes[:].bitcast(FP8X4), scales=z_plane[:],
                in_=grouped_z[start][:].rearrange("p c t -> p (c t)"),
            )
            per_bank = 512 // width
            sums[start] = []
            for first in range(0, N // P, per_bank):
                count = min(per_bank, N // P - first)
                y1 = psum.tile([P, count, width], F32, name="y1", tag="product", bufs=4)
                y2 = psum.tile([P, count, width], F32, name="y2", tag="sum", bufs=4)
                for g in range(count):
                    n0 = (first + g) * P
                    nc.tensor.matmul_mx(
                        out=y2[:, g, :], lhsT=w4_codes[:, 2 * n0 : 2 * (n0 + P)].bitcast(FP4X4),
                        lhsT_scale=w4_plane[:, n0 : n0 + P], rhs=z_codes[:].bitcast(FP8X4), rhs_scale=z_plane[:],
                        start=True, stop=True,
                    )
                for g in range(count):
                    n0 = (first + g) * P
                    nc.tensor.matmul_mx(
                        out=y1[:, g, :], lhsT=w3_codes[:, n0 : n0 + P].bitcast(FP8X4),
                        lhsT_scale=w3_plane[:, n0 : n0 + P], rhs=z_codes[:].bitcast(FP8X4), rhs_scale=z_plane[:],
                        start=True, stop=True,
                    )
                y2_plus = ring.tile([P, count, width], F32, name="y2_plus", bufs=4)
                nc.scalar.activation(out=y2_plus[:], in_=y2[:], func=ACT.Copy, scale=1.0, bias=1.0)
                sums[start].append((first, count, y1, y2_plus))

        def finish(start, width):
            result = ring.tile([P, N // P, width], F32, name="result")
            for first, count, y1, y2_plus in sums[start]:
                nc.vector.tensor_tensor(result[:, first : first + count, :], y1[:], y2_plus[:], ALU.mult)
            nc.sync.dma_start(out=out_rows[:, :, start : start + width], in_=result[:])

        starts = [sum(CHUNKS[:c]) for c in range(len(CHUNKS))]
        chunks = list(zip(starts, CHUNKS))
        for step in range(len(chunks) + 2):
            if step < len(chunks):
                get(*chunks[step], nc.scalar.copy if step + 1 < len(chunks) else nc.vector.tensor_copy)
            if 0 <= step - 1 < len(chunks):
                project(*chunks[step - 1])
            if 0 <= step - 2 < len(chunks):
                finish(*chunks[step - 2])
